import numpy as np, ml_dtypes
CORES = [97,101,225,229,353,357,481,485]
N = 8
TK = 32
def setup_inputs(rng):
    x = rng.standard_normal((N, 128, TK), dtype=np.float32).astype(ml_dtypes.bfloat16); w1 = (rng.standard_normal((N, 128, 128), dtype=np.float32) / 8).astype(ml_dtypes.bfloat16)
    wa = np.concatenate(list(w1.astype(np.float64)), axis=1)
    for r in range(N):
        while True:
            near = (np.abs(wa.T @ x[r].astype(np.float64)) < 2e-4).any(axis=0)
            if not near.any(): break
            x[r][:, near] = rng.standard_normal((128, int(near.sum())), dtype=np.float32).astype(ml_dtypes.bfloat16)
    return {"x": x, "dy": rng.standard_normal((N, 128, TK), dtype=np.float32).astype(ml_dtypes.bfloat16), "w1": w1, "w2t": (rng.standard_normal((N, 128, 128), dtype=np.float32) / 8).astype(ml_dtypes.bfloat16)}
def setup_inputs_big(rng):
    d = setup_inputs(rng)
    for k in ("x", "dy", "w1", "w2t"): d[k] = (d[k].astype(np.float32) * 1024.0).astype(d[k].dtype)
    return d
def setup_inputs_small(rng):
    d = setup_inputs(rng)
    for k in ("x", "dy", "w1", "w2t"): d[k] = (d[k].astype(np.float32) * (1 / 1024.0)).astype(d[k].dtype)
    return d
def setup_inputs_apart(rng):
    d = setup_inputs(rng)
    f = (10.0 ** rng.permutation(np.linspace(-1.5, 1.5, N))).astype(np.float32).reshape(N, 1, 1)
    for k in ("x", "dy", "w1", "w2t"): d[k] = (d[k].astype(np.float32) * f).astype(d[k].dtype)
    return d
def reference(x, dy, w1, w2t):
    X, DY, W1, W2T = x.astype(np.float64), dy.astype(np.float64), w1.astype(np.float64), w2t.astype(np.float64)
    dx = np.zeros((N, 128, TK))
    for r in range(N):
        for j in range(N):
            dx[r] += W1[j] @ ((W1[j].T @ X[r] > 0) * (W2T[j].T @ DY[r]))
    return {"dx": dx.astype(ml_dtypes.bfloat16)}

from concourse.bass import DstId, RemoteDMATransfer
from concourse.mybir import AluOpType, ActivationFunctionType

TK = 32
NT = 4 * TK
D = 128

SCRATCH = {
    "tok": ("sbuf", [128, 4, 2 * TK], "bfloat16"),
    "wown": ("sbuf", [128, 2 * D], "bfloat16"),
    "wgot": ("sbuf", [128, 2 * D], "bfloat16"),
    "ident": ("sbuf", [128, D], "bfloat16"),
    "wta": ("sbuf", [128, D], "bfloat16"),
    "wtb": ("sbuf", [128, D], "bfloat16"),
    "ma": ("sbuf", [128, NT], "bfloat16"),
    "mb": ("sbuf", [128, NT], "bfloat16"),
    "ga": ("sbuf", [128, NT], "bfloat16"),
    "gb": ("sbuf", [128, NT], "bfloat16"),
    "part": ("sbuf", [128, 3, TK], "bfloat16"),
    "rcv": ("sbuf", [128, 3, TK], "bfloat16"),
    "acc1": ("sbuf", [128, TK], "float32"),
    "acc2": ("sbuf", [128, TK], "float32"),
    "res": ("sbuf", [128, TK], "bfloat16"),
    "za": ("psum", [128, 512], "float32"),
    "ua": ("psum", [128, 512], "float32"),
    "zb": ("psum", [128, 512], "float32"),
    "ub": ("psum", [128, 512], "float32"),
    "ta": ("psum", [128, 512], "float32"),
    "tb": ("psum", [128, 512], "float32"),
    "dxp": ("psum", [128, 512], "float32"),
}
SEMAPHORES = ["tokld", "wld", "ones", "idn", "tokin", "win", "p1", "p2", "p3", "loc",
              "sta", "stb", "sza", "sua", "szb", "sub", "cta", "ctb", "sma", "smb", "sga", "sgb",
              "sdx", "conv", "a1", "a2", "sres", "stored"]


def _bits(m):
    return [b for b in range(m.bit_length()) if (m >> b) & 1]


def _mask(bs):
    return sum(1 << b for b in bs)


def rank_program(g, core, T, topo):
    if T.rank_of(core) is None:
        return
    S = T.sem
    others = [c for c in T.cores if c != core]
    here = (topo.host(core), topo.chip(core))
    peer = [c for c in others if (topo.host(c), topo.chip(c)) == here][0]
    plane = [c for c in others if topo.same_plane(core, c)]
    cable = [c for c in others if topo.may_write(core, c) and topo.rack(topo.host(c)) != topo.rack(topo.host(core))]
    wside, tside = plane, cable
    wdst = [c for c in wside if topo.die(c) == topo.die(core)][0]
    far = sorted(tside, key=lambda c: topo.die(c) != topo.die(core))

    off = _bits(topo.mask(core, wdst) & topo.mask(core, far[0]) & topo.mask(core, far[1]))
    chip_only = [b for b in _bits(topo.mask(core, peer)) if b not in off]
    m_off = _mask(off)
    n_off = len(off)
    on = chip_only[:4]
    m_on, n_on = _mask(on), len(on)
    half = n_off // 2
    m_lo, m_hi = _mask(off[:half]), _mask(off[half:])

    def dst(c):
        rid, pid = topo.addr(c, core)
        return DstId(rid=rid, pnc=pid)

    g.sync.dma_start(T.tok[:, 0, 0:TK], T.x[:]).then_inc(S.tokld, 16)
    g.scalar.dma_start(T.tok[:, 0, TK:2 * TK], T.dy[:]).then_inc(S.tokld, 16)
    g.sync.dma_start(T.wown[:, 0:D], T.w1[:]).then_inc(S.wld, 16)
    g.scalar.dma_start(T.wown[:, D:2 * D], T.w2t[:]).then_inc(S.wld, 16)

    g.vector.memset(T.ident[:], 1.0).then_inc(S.ones, 1)
    g.wait_ge(S.ones, 1)
    g.affine_select(T.ident[:], T.ident[:], [[-1, D]], AluOpType.is_equal, 0.0, 0, 1).then_inc(S.idn, 1)

    g.wait_ge(S.tokld, 32)
    g.remote_dma_fused([
        RemoteDMATransfer(dst_ids=[dst(far[0]), dst(far[1])], dma_engine_mask=m_off, remote_sem=S.tokin,
                          srcs=[T.tok[:, 0]], dsts=[T.tok[:, 2], T.tok[:, 3]]),
        RemoteDMATransfer(dst_ids=[dst(peer)], dma_engine_mask=m_on, remote_sem=S.tokin,
                          srcs=[T.tok[:, 0]], dsts=[T.tok[:, 1]]),
    ], local_sem=S.loc)
    g.wait_ge(S.wld, 32)
    rid, pid = topo.addr(wdst, core)
    g.remote_dma(T.wgot[:], T.wown[:], S.win, S.loc, pid, rid, m_off)

    te, ve, se = g.tensor, g.vector, g.scalar
    xs, dys = T.tok[:, :, 0:TK], T.tok[:, :, TK:2 * TK]
    te.wait_ge(S.wld, 32)
    te.wait_ge(S.idn, 1)
    te.matmul(T.ta[:, 0:D], T.wown[:, 0:D], T.ident[:], True, True).then_inc(S.sta, 1)
    te.wait_ge(S.tokld, 32)
    te.wait_ge(S.tokin, 2 * n_off + n_on)
    te.matmul(T.za[:, 0:NT], T.wown[:, 0:D], xs, True, True).then_inc(S.sza, 1)
    te.matmul(T.ua[:, 0:NT], T.wown[:, D:2 * D], dys, True, True).then_inc(S.sua, 1)
    te.wait_ge(S.win, n_off)
    te.matmul(T.tb[:, 0:D], T.wgot[:, 0:D], T.ident[:], True, True).then_inc(S.stb, 1)
    te.matmul(T.zb[:, 0:NT], T.wgot[:, 0:D], xs, True, True).then_inc(S.szb, 1)
    te.matmul(T.ub[:, 0:NT], T.wgot[:, D:2 * D], dys, True, True).then_inc(S.sub, 1)
    te.wait_ge(S.cta, 1)
    te.wait_ge(S.sga, 1)
    te.matmul(T.dxp[:, 0:NT], T.wta[:], T.ga[:], True, False)
    te.wait_ge(S.ctb, 1)
    te.wait_ge(S.sgb, 1)
    te.matmul(T.dxp[:, 0:NT], T.wtb[:], T.gb[:], False, True).then_inc(S.sdx, 1)

    se.wait_ge(S.sta, 1)
    se.activation(T.wta[:], T.ta[:, 0:D], ActivationFunctionType.Copy).then_inc(S.cta, 1)
    se.wait_ge(S.stb, 1)
    se.activation(T.wtb[:], T.tb[:, 0:D], ActivationFunctionType.Copy).then_inc(S.ctb, 1)

    for z, u, m, gg, sz, su, sm, sg in ((T.za, T.ua, T.ma, T.ga, S.sza, S.sua, S.sma, S.sga),
                                        (T.zb, T.ub, T.mb, T.gb, S.szb, S.sub, S.smb, S.sgb)):
        ve.wait_ge(sz, 1)
        ve.tensor_scalar(m[:], z[:, 0:NT], 0.0, None, AluOpType.is_gt).then_inc(sm, 1)
        ve.wait_ge(su, 1)
        ve.wait_ge(sm, 1)
        ve.tensor_tensor(gg[:], m[:], u[:, 0:NT], AluOpType.mult).then_inc(sg, 1)
    ve.wait_ge(S.sdx, 1)
    ve.tensor_copy(T.part[:, :, :], T.dxp[:, TK:NT]).then_inc(S.conv, 1)

    g.wait_ge(S.conv, 1)
    g.remote_dma_fused([
        RemoteDMATransfer(dst_ids=[dst(far[0])], dma_engine_mask=m_lo, remote_sem=S.p2,
                          srcs=[T.part[:, 1]], dsts=[T.rcv[:, 1]]),
        RemoteDMATransfer(dst_ids=[dst(far[1])], dma_engine_mask=m_hi, remote_sem=S.p3,
                          srcs=[T.part[:, 2]], dsts=[T.rcv[:, 2]]),
        RemoteDMATransfer(dst_ids=[dst(peer)], dma_engine_mask=m_on, remote_sem=S.p1,
                          srcs=[T.part[:, 0]], dsts=[T.rcv[:, 0]]),
    ], local_sem=S.loc)

    ve.wait_ge(S.p1, n_on)
    ve.tensor_tensor(T.acc1[:], T.rcv[:, 0], T.dxp[:, 0:TK], AluOpType.add).then_inc(S.a1, 1)
    ve.wait_ge(S.p2, half)
    ve.wait_ge(S.a1, 1)
    ve.tensor_tensor(T.acc2[:], T.acc1[:], T.rcv[:, 1], AluOpType.add).then_inc(S.a2, 1)
    ve.wait_ge(S.p3, n_off - half)
    ve.wait_ge(S.a2, 1)
    ve.tensor_tensor(T.res[:], T.acc2[:], T.rcv[:, 2], AluOpType.add).then_inc(S.sres, 1)
    g.sync.wait_ge(S.sres, 1)
    g.sync.dma_start(T.dx[:], T.res[:]).then_inc(S.stored, 16)
    g.sync.wait_ge(S.stored, 16)

    g.wait_ge(S.loc, (n_off + n_on) + n_off + (n_off + n_on))
